import numpy as np
import ml_dtypes


def mxq(x, axis, fmt="e4m3"):
    dtype, down = {"e4m3": (ml_dtypes.float8_e4m3fn, 7), "e5m2": (ml_dtypes.float8_e5m2, 14)}[fmt]
    v = np.moveaxis(np.asarray(x, np.float32).astype(ml_dtypes.bfloat16).astype(np.float64), axis, -1)
    blocks = v.reshape(v.shape[:-1] + (-1, 32))
    amax = np.abs(blocks).max(-1, keepdims=True)
    byte = np.maximum(np.where(amax > 0, np.frexp(amax)[1] - 1 + 127, 0) - down, 1)
    scale = np.exp2(byte - 127.0)
    codes = (blocks / scale).astype(np.float32).astype(dtype).astype(np.float64)
    return np.moveaxis((codes * scale).reshape(v.shape), -1, axis)


WIDE = False


def mx_kscale(k, group=512):
    if not WIDE:
        return np.ones(k)
    levels = np.array([10, -10, 5, -5, 0])
    if group != 512:
        return np.exp2(np.random.permutation(np.resize(levels, k // group))).repeat(group)
    if k % 512:
        return np.exp2(np.random.permutation(np.resize(levels, k // 32))).repeat(32)
    a = np.empty((k // 512, 16))
    for p in range(k // 512):
        a[p, :8] = np.random.permutation(np.resize(levels, 8))
        for g in range(8):
            far = levels[np.abs(levels - a[p, g]) >= 10]
            a[p, g + 8] = far[np.random.randint(len(far))]
    return np.exp2(a.ravel()).repeat(32)


def f64(x):
    return np.asarray(x).astype(np.float64)


def striped(idx):
    return np.tile(np.asarray(idx).reshape(-1, 16).T, (8, 1)).astype(np.uint16)


def unstriped(offs):
    return offs[:16].T.reshape(-1).astype(np.int64)


H, KV, D, NQ, N = 2, 2, 256, 512, 1024


def setup_inputs():
    n = np.random.standard_normal
    s = mx_kscale(D, 0)[:, None]
    u = mx_kscale(N)
    t = np.random.uniform(0.5, 2.0, N) * u
    v = n((KV, N, 128))
    v[:, :, 127] = 1.0
    return {
        "qT": (n((H, D, NQ)) * s * (0.70 / np.sqrt(D))).astype(np.float32),
        "kT": (n((KV, D, N)) / s).astype(np.float32),
        "t": t.reshape(N, 1).astype(np.float32),
        "v": (v / t[:, None]).astype(np.float32),
        "mask": (np.arange(N)[:, None] <= np.sort(np.random.randint(N // 4, N, NQ))[None, :]).astype(np.float32),
        "og": n((H, NQ, 128)).astype(np.float32),
    }


def reference(qT, kT, t, v, mask, og):
    a = mxq(f64(kT), 1, "e4m3").transpose(0, 2, 1) @ mxq(f64(qT), 1, "e4m3")
    p = np.square(np.maximum(a, 0.0))
    p = p * f64(mask)
    w = p * f64(t)
    y = mxq(w, 1, "e4m3").transpose(0, 2, 1) @ mxq(f64(v), 1, "e4m3")
    y = y / (y[:, :, 127:128] + 1.0)
    y = y / (1.0 + np.exp(-f64(og)))
    return y

@@ -1,0 +1,319 @@
+from contextlib import ExitStack
+
+import concourse.mybir as mybir
+
+H, D, NQ, N, E = 2, 256, 512, 1024, 128
+FLOPS = 2 * H * D * N * NQ + 2 * H * N * NQ * E
+
+F32 = mybir.dt.float32
+BF16 = mybir.dt.bfloat16
+U32 = mybir.dt.uint32
+U8 = mybir.dt.uint8
+FP8X4 = mybir.dt.float8_e4m3fn_x4
+ALU = mybir.AluOpType
+ACT = mybir.ActivationFunctionType
+
+P = 128
+PACK = 4
+ROWS = D // PACK
+TOK = P * PACK
+PASSES = N // TOK
+QC = 128
+CHUNKS = NQ // QC
+HALF = NQ // 2
+RUN = 4
+
+
+def tile_rows_a_relu2_mask_gate_kernel(tc, qT, kT, t, v, mask, og, out):
+    nc = tc.nc
+    with ExitStack() as ctx:
+        keep = ctx.enter_context(tc.tile_pool(name="keep", bufs=1))
+        work = ctx.enter_context(tc.tile_pool(name="work", bufs=4))
+        psum = ctx.enter_context(tc.psum_pool(name="psum", bufs=1))
+        ctx.enter_context(tc.manual_schedule())
+
+        def load(name, shape, src):
+            tile = keep.tile(shape, F32, name=name, align_bytes=64)
+            nc.sync.dma_start(out=tile[:], in_=src)
+            return tile
+
+        k_src = kT.rearrange("h (p j) n -> (h p) j n", j=PACK)
+        q_src = qT.rearrange("h (p j) n -> (h p) j n", j=PACK)
+
+        def load_k(g):
+            return load("k_raw%d" % g, [P, PACK, TOK], k_src[:, :, g * TOK:(g + 1) * TOK])
+
+        def load_q(a):
+            return load("q_raw%d" % a, [P, PACK, HALF], q_src[:, :, a * HALF:(a + 1) * HALF])
+
+        def load_mask(g, a):
+            rows = mask[g * TOK:(g + 1) * TOK, :].rearrange("(p j) n -> p j n", j=PACK)
+            return load("m_raw%d%d" % (g, a), [P, PACK, HALF], rows[:, :, a * HALF:(a + 1) * HALF])
+
+        def load_v(g):
+            rows = v[:, g * TOK:(g + 1) * TOK, :].rearrange("h (p j) e -> p h (j e)", j=PACK)
+            return load("v_raw%d" % g, [P, H, PACK * E], rows)
+
+        def load_og(h, c0, c1):
+            rows = og[h, c0 * QC:c1 * QC, :].rearrange("(c p) e -> p c e", p=P)
+            return load("og_raw%d%d" % (h, c0), [P, c1 - c0, E], rows)
+
+        k_raw, q_raw, m_raw, v_raw, og_raw = {}, {}, {}, {}, {}
+        t_raw = load("t_raw", [P, PASSES, PACK], t.rearrange("(g p j) o -> p g (j o)", p=P, j=PACK))
+        og_raw[0, 0] = load_og(0, 0, 1)
+        k_raw[0] = load_k(0)
+        q_raw[0] = load_q(0)
+        m_raw[0, 0] = load_mask(0, 0)
+        q_raw[1] = load_q(1)
+        m_raw[0, 1] = load_mask(0, 1)
+        v_raw[0] = load_v(0)
+        k_raw[1] = load_k(1)
+        m_raw[1, 0] = load_mask(1, 0)
+        v_raw[1] = load_v(1)
+        m_raw[1, 1] = load_mask(1, 1)
+        og_raw[0, 1] = load_og(0, 1, CHUNKS)
+        og_raw[1, 0] = load_og(1, 0, CHUNKS)
+
+        gates = {}
+
+        def sigmoid(h, c0):
+            src = og_raw[h, c0]
+            gate = keep.tile(list(src.shape), F32, name="gate%d%d" % (h, c0))
+            nc.scalar.activation(out=gate[:], in_=src[:], func=ACT.Sigmoid)
+            for c in range(src.shape[1]):
+                gates[h, c0 + c] = gate[:, c, :]
+
+        t_all = t_raw[:].rearrange("p g j -> p (g j)")
+        t_abs = keep.tile([P, PASSES * PACK], F32)
+        t_sign = keep.tile([P, PASSES * PACK], F32)
+        guess = keep.tile([P, PASSES * PACK], F32)
+        inv_guess = keep.tile([P, PASSES * PACK], F32)
+        half_ratio = keep.tile([P, PASSES * PACK], F32)
+        t_root = keep.tile([P, PASSES * PACK], F32)
+        nc.vector.scalar_tensor_tensor(out=t_abs[:], in0=t_all, scalar=-1.0, in1=t_all, op0=ALU.mult, op1=ALU.max)
+        nc.scalar.activation(out=guess[:], in_=t_abs[:], func=ACT.Sqrt)
+        nc.scalar.activation(out=t_sign[:], in_=t_all, func=ACT.Sign)
+        sigmoid(0, 0)
+        nc.vector.reciprocal(out=inv_guess[:], in_=guess[:])
+        nc.vector.scalar_tensor_tensor(out=half_ratio[:], in0=inv_guess[:], scalar=0.5, in1=t_abs[:], op0=ALU.mult, op1=ALU.mult)
+        nc.vector.scalar_tensor_tensor(out=t_root[:], in0=guess[:], scalar=0.5, in1=half_ratio[:], op0=ALU.mult, op1=ALU.add)
+
+        def copy_on(engine, dst, src):
+            if engine == "V":
+                nc.vector.tensor_copy(out=dst, in_=src)
+            else:
+                nc.scalar.copy(out=dst, in_=src)
+
+        def quantize(name, packed):
+            width = packed.shape[1] // PACK
+            codes = keep.tile([P, width], U32, name=name + "_codes", align_bytes=64)
+            scales = keep.tile([P, width], U8, name=name + "_scales", align_bytes=64)
+            nc.vector.quantize_mx(out=codes[:].bitcast(FP8X4), scales=scales[:], in_=packed)
+            return codes, scales
+
+        k_packed, q_packed, v_packed = {}, {}, {}
+        k_mx, q_mx, v_mx, w_mx = {}, {}, {}, {}
+        for g in range(PASSES):
+            k_packed[g] = keep.tile([P, PACK, P, PACK], BF16, name="k_packed%d" % g, align_bytes=64)
+            v_packed[g] = keep.tile([P, H, E, PACK], BF16, name="v_packed%d" % g, align_bytes=64)
+
+        def pack_k(engine, g, s0, s1):
+            dst = k_packed[g][:, :, s0:s1, :].rearrange("p r s j -> p s j r")
+            src = k_raw[g][:, :, s0 * PACK:s1 * PACK].rearrange("p j (s r) -> p s j r", r=PACK)
+            copy_on(engine, dst, src)
+
+        def quant_k(g):
+            k_mx[g] = quantize("k%d" % g, k_packed[g][:].rearrange("p r s j -> p (r s j)"))
+
+        def pack_q(engine, a):
+            q_packed[a] = keep.tile([P, HALF, PACK], BF16, name="q_packed%d" % a, align_bytes=64)
+            dst = q_packed[a][:].rearrange("p (c i) j -> p c j i", i=RUN)
+            src = q_raw[a][:].rearrange("p j (c i) -> p c j i", i=RUN)
+            copy_on(engine, dst, src)
+
+        def quant_q(a):
+            q_mx[a] = quantize("q%d" % a, q_packed[a][:].rearrange("p n j -> p (n j)"))
+
+        def pack_v(g, h):
+            dst = v_packed[g][:, h, :, :].rearrange("p (c i) j -> p c j i", i=RUN)
+            src = v_raw[g][:, h, :].rearrange("p (j c i) -> p c j i", j=PACK, i=RUN)
+            signs = t_sign[:, g * PACK:(g + 1) * PACK].unsqueeze(1).unsqueeze(3).to_broadcast([P, E // RUN, PACK, RUN])
+            nc.vector.tensor_tensor(out=dst, in0=src, in1=signs, op=ALU.mult)
+
+        def quant_v(g):
+            v_mx[g] = quantize("v%d" % g, v_packed[g][:].rearrange("p h e j -> p (h e j)"))
+
+        rooted = {}
+
+        def scale_mask(engine, g, c):
+            dst = keep.tile([P, PACK, QC], F32, name="rooted%d%d" % (g, c))
+            a, off = divmod(c * QC, HALF)
+            for j in range(PACK):
+                src = m_raw[g, a][:, j, off:off + QC]
+                root = t_root[:, g * PACK + j:g * PACK + j + 1]
+                if engine == "V":
+                    nc.vector.tensor_scalar(out=dst[:, j, :], in0=src, scalar1=root, scalar2=None, op0=ALU.mult)
+                else:
+                    nc.scalar.activation(out=dst[:, j, :], in_=src, func=ACT.Copy, scale=root)
+            rooted[g, c] = dst
+
+        banks, masked, weights = {}, {}, {}
+
+        def scores(g, c):
+            a, off = divmod(c * QC, HALF)
+            for h in range(H):
+                banks[g, c, h] = psum.tile([P, PACK, QC], F32, name="scores%d" % h, bufs=3)
+            for j in range(PACK):
+                for h in range(H):
+                    rows = slice(h * ROWS, (h + 1) * ROWS)
+                    nc.tensor.matmul_mx(
+                        out=banks[g, c, h][:, j, :],
+                        lhsT=k_mx[g][0][rows, j * P:(j + 1) * P].bitcast(FP8X4),
+                        lhsT_scale=k_mx[g][1][rows, j * P:(j + 1) * P],
+                        rhs=q_mx[a][0][rows, off:off + QC].bitcast(FP8X4),
+                        rhs_scale=q_mx[a][1][rows, off:off + QC],
+                        start=True,
+                        stop=True,
+                    )
+
+        def clip(g, c, heads):
+            u = work.tile([P, PACK, len(heads) * QC], F32, name="masked")
+            for i, h in enumerate(heads):
+                nc.vector.scalar_tensor_tensor(
+                    out=u[:, :, i * QC:(i + 1) * QC], in0=banks[g, c, h][:], scalar=0.0, in1=rooted[g, c][:],
+                    op0=ALU.max, op1=ALU.mult,
+                )
+            masked[g, c, heads] = u
+
+        def square(g, c, heads):
+            w = work.tile([P, len(heads) * QC, PACK], BF16, name="weights", align_bytes=64)
+            nc.scalar.activation(
+                out=w[:].rearrange("p (c i) j -> p c j i", i=RUN),
+                in_=masked[g, c, heads][:].rearrange("p j (c i) -> p c j i", i=RUN),
+                func=ACT.Square,
+            )
+            weights[g, c, heads] = w
+
+        def quant_w(g, c, heads):
+            codes, scales = quantize("w%d%d%d" % (g, c, heads[0]), weights[g, c, heads][:].rearrange("p n j -> p (n j)"))
+            for i, h in enumerate(heads):
+                w_mx[g, c, h] = (codes[:, i * QC:(i + 1) * QC], scales[:, i * QC:(i + 1) * QC])
+
+        sums, dens, invs = {}, {}, {}
+
+        def mix(c, heads):
+            y = psum.tile([P, len(heads), E], F32, name="sums", bufs=2)
+            for i, h in enumerate(heads):
+                for g in range(PASSES):
+                    nc.tensor.matmul_mx(
+                        out=y[:, i, :],
+                        lhsT=w_mx[g, c, h][0].bitcast(FP8X4),
+                        lhsT_scale=w_mx[g, c, h][1],
+                        rhs=v_mx[g][0][:, h * E:(h + 1) * E].bitcast(FP8X4),
+                        rhs_scale=v_mx[g][1][:, h * E:(h + 1) * E],
+                        start=(g == 0),
+                        stop=(g == PASSES - 1),
+                    )
+            sums[c, heads] = y
+
+        def denominator(c, heads):
+            den = work.tile([P, len(heads)], F32, name="den")
+            nc.vector.tensor_scalar(out=den[:], in0=sums[c, heads][:, :, E - 1], scalar1=1.0, scalar2=None, op0=ALU.add)
+            dens[c, heads] = den
+
+        def invert(c, heads):
+            inv = work.tile([P, len(heads)], F32, name="inv")
+            nc.vector.reciprocal(out=inv[:], in_=dens[c, heads][:])
+            invs[c, heads] = inv
+
+        def finish(c, heads):
+            res = work.tile([P, len(heads), E], F32, name="res")
+            for i, h in enumerate(heads):
+                nc.vector.scalar_tensor_tensor(
+                    out=res[:, i, :], in0=sums[c, heads][:, i, :], scalar=invs[c, heads][:, i:i + 1], in1=gates[h, c],
+                    op0=ALU.mult, op1=ALU.mult,
+                )
+            dst = out[heads[0]:heads[-1] + 1, c * QC:(c + 1) * QC, :].rearrange("h p e -> p h e")
+            nc.sync.dma_start(out=dst, in_=res[:])
+
+        both = (0, 1)
+        pack_k("V", 0, 0, P)
+        pack_q("S", 0)
+        quant_k(0)
+        quant_q(0)
+        scores(0, 0)
+        scores(0, 1)
+        scale_mask("V", 0, 0)
+        scale_mask("S", 0, 1)
+        pack_q("S", 1)
+        clip(0, 0, both)
+        square(0, 0, both)
+        clip(0, 1, both)
+        quant_q(1)
+        scores(0, 2)
+        scores(0, 3)
+        scale_mask("S", 0, 2)
+        quant_w(0, 0, both)
+        square(0, 1, both)
+        pack_v(0, 0)
+        pack_v(0, 1)
+        scale_mask("S", 0, 3)
+        clip(0, 2, both)
+        quant_v(0)
+        quant_w(0, 1, both)
+        pack_k("S", 1, 0, P // 2)
+        pack_k("S", 1, P // 2, P)
+        clip(0, 3, both)
+        square(0, 2, both)
+        square(0, 3, both)
+        scale_mask("V", 1, 0)
+        quant_k(1)
+        scores(1, 0)
+        scores(1, 1)
+        pack_v(1, 0)
+        pack_v(1, 1)
+        scale_mask("S", 1, 1)
+        clip(1, 0, both)
+        scores(1, 2)
+        square(1, 0, both)
+        quant_w(0, 2, both)
+        quant_v(1)
+        quant_w(0, 3, both)
+        scale_mask("S", 1, 2)
+        clip(1, 1, both)
+        scores(1, 3)
+        quant_w(1, 0, both)
+        mix(0, both)
+        square(1, 1, both)
+        scale_mask("S", 1, 3)
+        sigmoid(1, 0)
+        clip(1, 2, both)
+        denominator(0, both)
+        quant_w(1, 1, both)
+        mix(1, both)
+        invert(0, both)
+        square(1, 2, both)
+        sigmoid(0, 1)
+        clip(1, 3, (0,))
+        finish(0, both)
+        square(1, 3, (0,))
+        clip(1, 3, (1,))
+        square(1, 3, (1,))
+        denominator(1, both)
+        quant_w(1, 2, both)
+        invert(1, both)
+        finish(1, both)
+        mix(2, both)
+        quant_w(1, 3, (0,))
+        mix(3, (0,))
+        denominator(2, both)
+        quant_w(1, 3, (1,))
+        invert(2, both)
+        denominator(3, (0,))
+        finish(2, both)
+        mix(3, (1,))
+        invert(3, (0,))
+        denominator(3, (1,))
+        finish(3, (0,))
+        invert(3, (1,))
+        finish(3, (1,))

@@ -50,9 +50,9 @@ def tile_rows_a_relu2_mask_gate_kernel(tc, qT, kT, t, v, mask, og, out):
             rows = mask[g * TOK:(g + 1) * TOK, :].rearrange("(p j) n -> p j n", j=PACK)
             return load("m_raw%d%d" % (g, a), [P, PACK, HALF], rows[:, :, a * HALF:(a + 1) * HALF])
 
-        def load_v(g):
-            rows = v[:, g * TOK:(g + 1) * TOK, :].rearrange("h (p j) e -> p h (j e)", j=PACK)
-            return load("v_raw%d" % g, [P, H, PACK * E], rows)
+        def load_v(h):
+            rows = v[h].rearrange("(g p j) e -> p g (j e)", p=P, j=PACK)
+            return load("v_raw%d" % h, [P, PASSES, PACK * E], rows)
 
         def load_og(h, c0, c1):
             rows = og[h, c0 * QC:c1 * QC, :].rearrange("(c p) e -> p c e", p=P)
@@ -64,11 +64,11 @@ def tile_rows_a_relu2_mask_gate_kernel(tc, qT, kT, t, v, mask, og, out):
         k_raw[0] = load_k(0)
         q_raw[0] = load_q(0)
         m_raw[0, 0] = load_mask(0, 0)
-        q_raw[1] = load_q(1)
-        m_raw[0, 1] = load_mask(0, 1)
-        v_raw[0] = load_v(0)
         k_raw[1] = load_k(1)
         m_raw[1, 0] = load_mask(1, 0)
+        q_raw[1] = load_q(1)
+        v_raw[0] = load_v(0)
+        m_raw[0, 1] = load_mask(0, 1)
         v_raw[1] = load_v(1)
         m_raw[1, 1] = load_mask(1, 1)
         og_raw[0, 1] = load_og(0, 1, CHUNKS)
@@ -101,6 +101,8 @@ def tile_rows_a_relu2_mask_gate_kernel(tc, qT, kT, t, v, mask, og, out):
         def copy_on(engine, dst, src):
             if engine == "V":
                 nc.vector.tensor_copy(out=dst, in_=src)
+            elif engine == "G":
+                nc.gpsimd.tensor_scalar(out=dst, in0=src, scalar1=1.0, scalar2=0.0, op0=ALU.mult, op1=ALU.add)
             else:
                 nc.scalar.copy(out=dst, in_=src)
 
@@ -113,11 +115,13 @@ def tile_rows_a_relu2_mask_gate_kernel(tc, qT, kT, t, v, mask, og, out):
 
         k_packed, q_packed, v_packed = {}, {}, {}
         k_mx, q_mx, v_mx, w_mx = {}, {}, {}, {}
-        for g in range(PASSES):
-            k_packed[g] = keep.tile([P, PACK, P, PACK], BF16, name="k_packed%d" % g, align_bytes=64)
-            v_packed[g] = keep.tile([P, H, E, PACK], BF16, name="v_packed%d" % g, align_bytes=64)
+
+        def staging(key, shape, tag):
+            return keep.tile(shape, BF16, name="packed_%s" % key, tag=tag, align_bytes=64)
 
         def pack_k(engine, g, s0, s1):
+            if g not in k_packed:
+                k_packed[g] = staging("k%d" % g, [P, PACK, P, PACK], "stage_k%d" % g)
             dst = k_packed[g][:, :, s0:s1, :].rearrange("p r s j -> p s j r")
             src = k_raw[g][:, :, s0 * PACK:s1 * PACK].rearrange("p j (s r) -> p s j r", r=PACK)
             copy_on(engine, dst, src)
@@ -125,23 +129,30 @@ def tile_rows_a_relu2_mask_gate_kernel(tc, qT, kT, t, v, mask, og, out):
         def quant_k(g):
             k_mx[g] = quantize("k%d" % g, k_packed[g][:].rearrange("p r s j -> p (r s j)"))
 
-        def pack_q(engine, a):
-            q_packed[a] = keep.tile([P, HALF, PACK], BF16, name="q_packed%d" % a, align_bytes=64)
-            dst = q_packed[a][:].rearrange("p (c i) j -> p c j i", i=RUN)
-            src = q_raw[a][:].rearrange("p j (c i) -> p c j i", i=RUN)
+        def pack_q(engine, c0, c1, n0, n1, tag):
+            if c0 not in q_packed:
+                q_packed[c0] = staging("q%d" % c0, [P, (c1 - c0) * QC, PACK], tag)
+            a, off = divmod(c0 * QC, HALF)
+            dst = q_packed[c0][:, n0:n1, :].rearrange("p (c i) j -> p c j i", i=RUN)
+            src = q_raw[a][:, :, off + n0:off + n1].rearrange("p j (c i) -> p c j i", i=RUN)
             copy_on(engine, dst, src)
 
-        def quant_q(a):
-            q_mx[a] = quantize("q%d" % a, q_packed[a][:].rearrange("p n j -> p (n j)"))
+        def quant_q(c0, c1):
+            codes, scales = quantize("q%d" % c0, q_packed[c0][:].rearrange("p n j -> p (n j)"))
+            for c in range(c0, c1):
+                cols = slice((c - c0) * QC, (c - c0 + 1) * QC)
+                q_mx[c] = (codes, scales, cols)
 
-        def pack_v(g, h):
-            dst = v_packed[g][:, h, :, :].rearrange("p (c i) j -> p c j i", i=RUN)
-            src = v_raw[g][:, h, :].rearrange("p (j c i) -> p c j i", j=PACK, i=RUN)
-            signs = t_sign[:, g * PACK:(g + 1) * PACK].unsqueeze(1).unsqueeze(3).to_broadcast([P, E // RUN, PACK, RUN])
-            nc.vector.tensor_tensor(out=dst, in0=src, in1=signs, op=ALU.mult)
+        def pack_v(h, tag):
+            v_packed[h] = staging("v%d" % h, [P, PASSES, E, PACK], tag)
+            for g in range(PASSES):
+                dst = v_packed[h][:, g, :, :].rearrange("p (c i) j -> p c j i", i=RUN)
+                src = v_raw[h][:, g, :].rearrange("p (j c i) -> p c j i", j=PACK, i=RUN)
+                signs = t_sign[:, g * PACK:(g + 1) * PACK].unsqueeze(1).unsqueeze(3).to_broadcast([P, E // RUN, PACK, RUN])
+                nc.gpsimd.tensor_tensor(out=dst, in0=src, in1=signs, op=ALU.mult)
 
-        def quant_v(g):
-            v_mx[g] = quantize("v%d" % g, v_packed[g][:].rearrange("p h e j -> p (h e j)"))
+        def quant_v(h):
+            v_mx[h] = quantize("v%d" % h, v_packed[h][:].rearrange("p g e j -> p (g e j)"))
 
         rooted = {}
 
@@ -160,38 +171,41 @@ def tile_rows_a_relu2_mask_gate_kernel(tc, qT, kT, t, v, mask, og, out):
         banks, masked, weights = {}, {}, {}
 
         def scores(g, c):
-            a, off = divmod(c * QC, HALF)
+            q_codes, q_scales, cols = q_mx[c]
             for h in range(H):
-                banks[g, c, h] = psum.tile([P, PACK, QC], F32, name="scores%d" % h, bufs=3)
-            for j in range(PACK):
-                for h in range(H):
-                    rows = slice(h * ROWS, (h + 1) * ROWS)
+                bank = psum.tile([P, PACK, QC], F32, name="scores%d" % h, bufs=2)
+                rows = slice(h * ROWS, (h + 1) * ROWS)
+                for j in range(PACK):
                     nc.tensor.matmul_mx(
-                        out=banks[g, c, h][:, j, :],
+                        out=bank[:, j, :],
                         lhsT=k_mx[g][0][rows, j * P:(j + 1) * P].bitcast(FP8X4),
                         lhsT_scale=k_mx[g][1][rows, j * P:(j + 1) * P],
-                        rhs=q_mx[a][0][rows, off:off + QC].bitcast(FP8X4),
-                        rhs_scale=q_mx[a][1][rows, off:off + QC],
+                        rhs=q_codes[rows, cols].bitcast(FP8X4),
+                        rhs_scale=q_scales[rows, cols],
                         start=True,
                         stop=True,
                     )
+                banks[g, c, h] = bank
 
-        def clip(g, c, heads):
-            u = work.tile([P, PACK, len(heads) * QC], F32, name="masked")
+        def clip(g, c, heads, only=None):
+            if (g, c, heads) not in masked:
+                masked[g, c, heads] = keep.tile([P, PACK, len(heads) * QC], F32, name="masked%d%d%d" % (g, c, heads[0]))
+            u = masked[g, c, heads]
             for i, h in enumerate(heads):
-                nc.vector.scalar_tensor_tensor(
-                    out=u[:, :, i * QC:(i + 1) * QC], in0=banks[g, c, h][:], scalar=0.0, in1=rooted[g, c][:],
-                    op0=ALU.max, op1=ALU.mult,
-                )
-            masked[g, c, heads] = u
+                if only is None or h == only:
+                    nc.vector.scalar_tensor_tensor(
+                        out=u[:, :, i * QC:(i + 1) * QC], in0=banks[g, c, h][:], scalar=0.0, in1=rooted[g, c][:],
+                        op0=ALU.max, op1=ALU.mult,
+                    )
 
-        def square(g, c, heads):
-            w = work.tile([P, len(heads) * QC, PACK], BF16, name="weights", align_bytes=64)
-            nc.scalar.activation(
-                out=w[:].rearrange("p (c i) j -> p c j i", i=RUN),
-                in_=masked[g, c, heads][:].rearrange("p j (c i) -> p c j i", i=RUN),
-                func=ACT.Square,
-            )
+        def square(g, c, heads, engine="S"):
+            w = staging("w%d%d%d" % (g, c, heads[0]), [P, len(heads) * QC, PACK], "stage_w%d%d%d" % (g, c, heads[0]))
+            dst = w[:].rearrange("p (c i) j -> p c j i", i=RUN)
+            src = masked[g, c, heads][:].rearrange("p j (c i) -> p c j i", i=RUN)
+            if engine == "S":
+                nc.scalar.activation(out=dst, in_=src, func=ACT.Square)
+            else:
+                nc.vector.tensor_tensor(out=dst, in0=src, in1=src, op=ALU.mult)
             weights[g, c, heads] = w
 
         def quant_w(g, c, heads):
@@ -201,119 +215,132 @@ def tile_rows_a_relu2_mask_gate_kernel(tc, qT, kT, t, v, mask, og, out):
 
         sums, dens, invs = {}, {}, {}
 
-        def mix(c, heads):
-            y = psum.tile([P, len(heads), E], F32, name="sums", bufs=2)
-            for i, h in enumerate(heads):
+        def mix(unit):
+            y = psum.tile([P, len(unit), E], F32, name="sums", bufs=4)
+            for i, (c, h) in enumerate(unit):
                 for g in range(PASSES):
                     nc.tensor.matmul_mx(
                         out=y[:, i, :],
                         lhsT=w_mx[g, c, h][0].bitcast(FP8X4),
                         lhsT_scale=w_mx[g, c, h][1],
-                        rhs=v_mx[g][0][:, h * E:(h + 1) * E].bitcast(FP8X4),
-                        rhs_scale=v_mx[g][1][:, h * E:(h + 1) * E],
+                        rhs=v_mx[h][0][:, g * E:(g + 1) * E].bitcast(FP8X4),
+                        rhs_scale=v_mx[h][1][:, g * E:(g + 1) * E],
                         start=(g == 0),
                         stop=(g == PASSES - 1),
                     )
-            sums[c, heads] = y
+            sums[unit] = y
 
-        def denominator(c, heads):
-            den = work.tile([P, len(heads)], F32, name="den")
-            nc.vector.tensor_scalar(out=den[:], in0=sums[c, heads][:, :, E - 1], scalar1=1.0, scalar2=None, op0=ALU.add)
-            dens[c, heads] = den
+        def denominator(unit):
+            den = work.tile([P, len(unit)], F32, name="den")
+            nc.vector.tensor_scalar(out=den[:], in0=sums[unit][:, :, E - 1], scalar1=1.0, scalar2=None, op0=ALU.add)
+            dens[unit] = den
 
-        def invert(c, heads):
-            inv = work.tile([P, len(heads)], F32, name="inv")
-            nc.vector.reciprocal(out=inv[:], in_=dens[c, heads][:])
-            invs[c, heads] = inv
+        def invert(unit):
+            inv = work.tile([P, len(unit)], F32, name="inv")
+            nc.vector.reciprocal(out=inv[:], in_=dens[unit][:])
+            invs[unit] = inv
 
-        def finish(c, heads):
-            res = work.tile([P, len(heads), E], F32, name="res")
-            for i, h in enumerate(heads):
+        def finish(unit):
+            res = keep.tile([P, len(unit), E], F32, name="res%d%d" % unit[0])
+            for i, (c, h) in enumerate(unit):
                 nc.vector.scalar_tensor_tensor(
-                    out=res[:, i, :], in0=sums[c, heads][:, i, :], scalar=invs[c, heads][:, i:i + 1], in1=gates[h, c],
+                    out=res[:, i, :], in0=sums[unit][:, i, :], scalar=invs[unit][:, i:i + 1], in1=gates[h, c],
                     op0=ALU.mult, op1=ALU.mult,
                 )
-            dst = out[heads[0]:heads[-1] + 1, c * QC:(c + 1) * QC, :].rearrange("h p e -> p h e")
+            (c0, h0), (c1, h1) = unit[0], unit[-1]
+            if h0 == h1:
+                dst = out[h0, c0 * QC:(c1 + 1) * QC, :].rearrange("(c p) e -> p c e", p=P)
+            else:
+                dst = out[:, c0 * QC:(c0 + 1) * QC, :].rearrange("h p e -> p h e")
             nc.sync.dma_start(out=dst, in_=res[:])
 
         both = (0, 1)
-        pack_k("V", 0, 0, P)
-        pack_q("S", 0)
+        early0, early1 = ((0, 0), (1, 0)), ((0, 1), (1, 1))
+        third, last0, last1 = ((2, 0), (2, 1)), ((3, 0),), ((3, 1),)
+        pack_k("V", 0, 0, 84)
+        pack_k("S", 0, 84, P)
         quant_k(0)
-        quant_q(0)
+        pack_q("S", 0, 1, 0, QC, "stage_q0")
+        pack_q("V", 1, 2, 0, QC, "stage_q1")
+        quant_q(0, 1)
         scores(0, 0)
+        quant_q(1, 2)
         scores(0, 1)
         scale_mask("V", 0, 0)
         scale_mask("S", 0, 1)
-        pack_q("S", 1)
-        clip(0, 0, both)
-        square(0, 0, both)
-        clip(0, 1, both)
-        quant_q(1)
-        scores(0, 2)
-        scores(0, 3)
-        scale_mask("S", 0, 2)
-        quant_w(0, 0, both)
-        square(0, 1, both)
-        pack_v(0, 0)
-        pack_v(0, 1)
-        scale_mask("S", 0, 3)
-        clip(0, 2, both)
-        quant_v(0)
-        quant_w(0, 1, both)
-        pack_k("S", 1, 0, P // 2)
-        pack_k("S", 1, P // 2, P)
-        clip(0, 3, both)
-        square(0, 2, both)
-        square(0, 3, both)
-        scale_mask("V", 1, 0)
+        clip(0, 0, (0,))
+        square(0, 0, (0,))
+        clip(0, 0, (1,))
+        square(0, 0, (1,))
+        clip(0, 1, both, 0)
+        pack_k("S", 1, 0, 44)
+        pack_k("V", 1, 44, P)
+        quant_w(0, 0, (0,))
         quant_k(1)
         scores(1, 0)
+        scale_mask("S", 1, 0)
+        clip(0, 1, both, 1)
         scores(1, 1)
-        pack_v(1, 0)
-        pack_v(1, 1)
+        pack_q("G", 2, 4, 0, 192, "stage_k1")
         scale_mask("S", 1, 1)
+        pack_q("S", 2, 4, 192, HALF, "stage_k1")
+        square(0, 1, both)
         clip(1, 0, both)
-        scores(1, 2)
+        quant_w(0, 0, (1,))
+        quant_q(2, 4)
+        scores(0, 2)
+        quant_w(0, 1, both)
+        pack_v(0, "stage_w010")
         square(1, 0, both)
+        scale_mask("S", 0, 2)
+        scale_mask("S", 0, 3)
+        clip(1, 1, both)
+        scores(0, 3)
+        square(1, 1, both)
+        clip(0, 2, both)
+        scores(1, 2)
+        square(0, 2, both)
+        scale_mask("S", 1, 2)
+        quant_w(1, 0, both)
+        quant_v(0)
+        quant_w(1, 1, both)
+        mix(early0)
+        pack_v(1, "stage_w110")
+        clip(0, 3, both)
+        scores(1, 3)
+        scale_mask("S", 1, 3)
+        sigmoid(0, 1)
+        square(0, 3, both)
+        denominator(early0)
+        clip(1, 2, both, 0)
+        invert(early0)
+        clip(1, 2, both, 1)
+        sigmoid(1, 0)
+        square(1, 2, both)
+        finish(early0)
         quant_w(0, 2, both)
         quant_v(1)
+        mix(early1)
         quant_w(0, 3, both)
-        scale_mask("S", 1, 2)
-        clip(1, 1, both)
-        scores(1, 3)
-        quant_w(1, 0, both)
-        mix(0, both)
-        square(1, 1, both)
-        scale_mask("S", 1, 3)
-        sigmoid(1, 0)
-        clip(1, 2, both)
-        denominator(0, both)
-        quant_w(1, 1, both)
-        mix(1, both)
-        invert(0, both)
-        square(1, 2, both)
-        sigmoid(0, 1)
         clip(1, 3, (0,))
-        finish(0, both)
-        square(1, 3, (0,))
         clip(1, 3, (1,))
-        square(1, 3, (1,))
-        denominator(1, both)
+        square(1, 3, (0,))
+        denominator(early1)
         quant_w(1, 2, both)
-        invert(1, both)
-        finish(1, both)
-        mix(2, both)
+        mix(third)
+        square(1, 3, (1,), "V")
+        invert(early1)
         quant_w(1, 3, (0,))
-        mix(3, (0,))
-        denominator(2, both)
+        mix(last0)
         quant_w(1, 3, (1,))
-        invert(2, both)
-        denominator(3, (0,))
-        finish(2, both)
-        mix(3, (1,))
-        invert(3, (0,))
-        denominator(3, (1,))
-        finish(3, (0,))
-        invert(3, (1,))
-        finish(3, (1,))
+        mix(last1)
+        denominator(third)
+        finish(early1)
+        invert(third)
+        denominator(last0)
+        denominator(last1)
+        finish(third)
+        invert(last0)
+        invert(last1)
+        finish(last0)
+        finish(last1)

@@ -32,9 +32,9 @@ def tile_rows_a_relu2_mask_gate_kernel(tc, qT, kT, t, v, mask, og, out):
         psum = ctx.enter_context(tc.psum_pool(name="psum", bufs=1))
         ctx.enter_context(tc.manual_schedule())
 
-        def load(name, shape, src):
+        def load(name, shape, src, queue=nc.sync):
             tile = keep.tile(shape, F32, name=name, align_bytes=64)
-            nc.sync.dma_start(out=tile[:], in_=src)
+            queue.dma_start(out=tile[:], in_=src)
             return tile
 
         k_src = kT.rearrange("h (p j) n -> (h p) j n", j=PACK)
@@ -54,9 +54,9 @@ def tile_rows_a_relu2_mask_gate_kernel(tc, qT, kT, t, v, mask, og, out):
             rows = v[h].rearrange("(g p j) e -> p g (j e)", p=P, j=PACK)
             return load("v_raw%d" % h, [P, PASSES, PACK * E], rows)
 
-        def load_og(h, c0, c1):
+        def load_og(h, c0, c1, queue=nc.sync):
             rows = og[h, c0 * QC:c1 * QC, :].rearrange("(c p) e -> p c e", p=P)
-            return load("og_raw%d%d" % (h, c0), [P, c1 - c0, E], rows)
+            return load("og_raw%d%d" % (h, c0), [P, c1 - c0, E], rows, queue)
 
         k_raw, q_raw, m_raw, v_raw, og_raw = {}, {}, {}, {}, {}
         t_raw = load("t_raw", [P, PASSES, PACK], t.rearrange("(g p j) o -> p g (j o)", p=P, j=PACK))
@@ -76,12 +76,11 @@ def tile_rows_a_relu2_mask_gate_kernel(tc, qT, kT, t, v, mask, og, out):
 
         gates = {}
 
-        def sigmoid(h, c0):
-            src = og_raw[h, c0]
-            gate = keep.tile(list(src.shape), F32, name="gate%d%d" % (h, c0))
-            nc.scalar.activation(out=gate[:], in_=src[:], func=ACT.Sigmoid)
-            for c in range(src.shape[1]):
-                gates[h, c0 + c] = gate[:, c, :]
+        def sigmoid(h, first, c0, c1):
+            gate = keep.tile([P, c1 - c0, E], F32, name="gate%d%d" % (h, c0))
+            nc.scalar.activation(out=gate[:], in_=og_raw[h, first][:, c0 - first:c1 - first, :], func=ACT.Sigmoid)
+            for c in range(c0, c1):
+                gates[h, c] = gate[:, c - c0, :]
 
         t_all = t_raw[:].rearrange("p g j -> p (g j)")
         t_abs = keep.tile([P, PASSES * PACK], F32)
@@ -93,7 +92,7 @@ def tile_rows_a_relu2_mask_gate_kernel(tc, qT, kT, t, v, mask, og, out):
         nc.vector.scalar_tensor_tensor(out=t_abs[:], in0=t_all, scalar=-1.0, in1=t_all, op0=ALU.mult, op1=ALU.max)
         nc.scalar.activation(out=guess[:], in_=t_abs[:], func=ACT.Sqrt)
         nc.scalar.activation(out=t_sign[:], in_=t_all, func=ACT.Sign)
-        sigmoid(0, 0)
+        sigmoid(0, 0, 0, 1)
         nc.vector.reciprocal(out=inv_guess[:], in_=guess[:])
         nc.vector.scalar_tensor_tensor(out=half_ratio[:], in0=inv_guess[:], scalar=0.5, in1=t_abs[:], op0=ALU.mult, op1=ALU.mult)
         nc.vector.scalar_tensor_tensor(out=t_root[:], in0=guess[:], scalar=0.5, in1=half_ratio[:], op0=ALU.mult, op1=ALU.add)
@@ -156,14 +155,16 @@ def tile_rows_a_relu2_mask_gate_kernel(tc, qT, kT, t, v, mask, og, out):
 
         rooted = {}
 
-        def scale_mask(engine, g, c):
-            dst = keep.tile([P, PACK, QC], F32, name="rooted%d%d" % (g, c))
+        def scale_mask(engine, g, c, tag=""):
+            dst = keep.tile([P, PACK, QC], F32, name="rooted%d%d" % (g, c), tag=tag, align_bytes=64)
             a, off = divmod(c * QC, HALF)
             for j in range(PACK):
                 src = m_raw[g, a][:, j, off:off + QC]
                 root = t_root[:, g * PACK + j:g * PACK + j + 1]
                 if engine == "V":
                     nc.vector.tensor_scalar(out=dst[:, j, :], in0=src, scalar1=root, scalar2=None, op0=ALU.mult)
+                elif engine == "G":
+                    nc.gpsimd.tensor_scalar(out=dst[:, j, :], in0=src, scalar1=root, scalar2=0.0, op0=ALU.mult, op1=ALU.add)
                 else:
                     nc.scalar.activation(out=dst[:, j, :], in_=src, func=ACT.Copy, scale=root)
             rooted[g, c] = dst
@@ -215,10 +216,12 @@ def tile_rows_a_relu2_mask_gate_kernel(tc, qT, kT, t, v, mask, og, out):
 
         sums, dens, invs = {}, {}, {}
 
-        def mix(unit):
-            y = psum.tile([P, len(unit), E], F32, name="sums", bufs=4)
+        def mix(unit, passes=range(PASSES)):
+            if unit not in sums:
+                sums[unit] = psum.tile([P, len(unit), E], F32, name="sums", bufs=4)
+            y = sums[unit]
             for i, (c, h) in enumerate(unit):
-                for g in range(PASSES):
+                for g in passes:
                     nc.tensor.matmul_mx(
                         out=y[:, i, :],
                         lhsT=w_mx[g, c, h][0].bitcast(FP8X4),
@@ -228,7 +231,6 @@ def tile_rows_a_relu2_mask_gate_kernel(tc, qT, kT, t, v, mask, og, out):
                         start=(g == 0),
                         stop=(g == PASSES - 1),
                     )
-            sums[unit] = y
 
         def denominator(unit):
             den = work.tile([P, len(unit)], F32, name="den")
@@ -278,20 +280,22 @@ def tile_rows_a_relu2_mask_gate_kernel(tc, qT, kT, t, v, mask, og, out):
         quant_w(0, 0, (0,))
         quant_k(1)
         scores(1, 0)
-        scale_mask("S", 1, 0)
+        scale_mask("S", 1, 1)
+        scale_mask("V", 1, 0)
         clip(0, 1, both, 1)
         scores(1, 1)
         pack_q("G", 2, 4, 0, 192, "stage_k1")
-        scale_mask("S", 1, 1)
         pack_q("S", 2, 4, 192, HALF, "stage_k1")
         square(0, 1, both)
-        clip(1, 0, both)
+        clip(1, 0, (0,))
+        square(1, 0, (0,))
+        clip(1, 0, (1,))
+        square(1, 0, (1,))
         quant_w(0, 0, (1,))
         quant_q(2, 4)
         scores(0, 2)
         quant_w(0, 1, both)
-        pack_v(0, "stage_w010")
-        square(1, 0, both)
+        pack_v(0, "stage_k1")
         scale_mask("S", 0, 2)
         scale_mask("S", 0, 3)
         clip(1, 1, both)
@@ -299,48 +303,51 @@ def tile_rows_a_relu2_mask_gate_kernel(tc, qT, kT, t, v, mask, og, out):
         square(1, 1, both)
         clip(0, 2, both)
         scores(1, 2)
-        square(0, 2, both)
         scale_mask("S", 1, 2)
-        quant_w(1, 0, both)
+        square(0, 2, both)
+        quant_w(1, 0, (0,))
+        quant_w(1, 0, (1,))
         quant_v(0)
         quant_w(1, 1, both)
         mix(early0)
-        pack_v(1, "stage_w110")
+        scale_mask("G", 1, 3, "stage_k1")
+        pack_v(1, "stage_v1")
         clip(0, 3, both)
         scores(1, 3)
-        scale_mask("S", 1, 3)
-        sigmoid(0, 1)
+        sigmoid(0, 1, 1, 2)
         square(0, 3, both)
-        denominator(early0)
-        clip(1, 2, both, 0)
-        invert(early0)
-        clip(1, 2, both, 1)
-        sigmoid(1, 0)
+        clip(1, 2, both)
         square(1, 2, both)
+        denominator(early0)
+        clip(1, 3, (0,))
+        invert(early0)
+        clip(1, 3, (1,))
         finish(early0)
-        quant_w(0, 2, both)
+        square(1, 3, (0,))
+        sigmoid(1, 0, 0, 2)
+        square(1, 3, (1,))
+        sigmoid(0, 1, 2, 4)
+        sigmoid(1, 0, 2, 4)
         quant_v(1)
         mix(early1)
-        quant_w(0, 3, both)
-        clip(1, 3, (0,))
-        clip(1, 3, (1,))
-        square(1, 3, (0,))
-        denominator(early1)
+        quant_w(0, 2, both)
         quant_w(1, 2, both)
         mix(third)
-        square(1, 3, (1,), "V")
-        invert(early1)
+        quant_w(0, 3, both)
         quant_w(1, 3, (0,))
         mix(last0)
+        mix(last1, (0,))
+        denominator(early1)
+        invert(early1)
         quant_w(1, 3, (1,))
-        mix(last1)
-        denominator(third)
+        mix(last1, (1,))
         finish(early1)
-        invert(third)
+        denominator(third)
         denominator(last0)
         denominator(last1)
-        finish(third)
+        invert(third)
         invert(last0)
         invert(last1)
+        finish(third)
         finish(last0)
         finish(last1)

@@ -67,8 +67,8 @@ def tile_rows_a_relu2_mask_gate_kernel(tc, qT, kT, t, v, mask, og, out):
         k_raw[1] = load_k(1)
         m_raw[1, 0] = load_mask(1, 0)
         q_raw[1] = load_q(1)
-        v_raw[0] = load_v(0)
         m_raw[0, 1] = load_mask(0, 1)
+        v_raw[0] = load_v(0)
         v_raw[1] = load_v(1)
         m_raw[1, 1] = load_mask(1, 1)
         og_raw[0, 1] = load_og(0, 1, CHUNKS)
@@ -282,6 +282,7 @@ def tile_rows_a_relu2_mask_gate_kernel(tc, qT, kT, t, v, mask, og, out):
         scores(1, 0)
         scale_mask("S", 1, 1)
         scale_mask("V", 1, 0)
+        quant_w(0, 0, (1,))
         clip(0, 1, both, 1)
         scores(1, 1)
         pack_q("G", 2, 4, 0, 192, "stage_k1")
@@ -291,63 +292,69 @@ def tile_rows_a_relu2_mask_gate_kernel(tc, qT, kT, t, v, mask, og, out):
         square(1, 0, (0,))
         clip(1, 0, (1,))
         square(1, 0, (1,))
-        quant_w(0, 0, (1,))
         quant_q(2, 4)
         scores(0, 2)
+        scale_mask("V", 0, 2)
         quant_w(0, 1, both)
-        pack_v(0, "stage_k1")
-        scale_mask("S", 0, 2)
+        quant_w(1, 0, (0,))
+        pack_v(0, "stage_w010")
+        pack_v(1, "stage_v1")
         scale_mask("S", 0, 3)
-        clip(1, 1, both)
+        clip(1, 1, (0,))
+        square(1, 1, (0,))
+        clip(1, 1, (1,))
+        square(1, 1, (1,))
         scores(0, 3)
-        square(1, 1, both)
-        clip(0, 2, both)
+        clip(0, 2, (0,))
+        square(0, 2, (0,))
+        clip(0, 2, (1,))
         scores(1, 2)
         scale_mask("S", 1, 2)
-        square(0, 2, both)
-        quant_w(1, 0, (0,))
-        quant_w(1, 0, (1,))
-        quant_v(0)
-        quant_w(1, 1, both)
-        mix(early0)
-        scale_mask("G", 1, 3, "stage_k1")
-        pack_v(1, "stage_v1")
+        scale_mask("S", 1, 3)
+        square(0, 2, (1,))
         clip(0, 3, both)
         scores(1, 3)
-        sigmoid(0, 1, 1, 2)
         square(0, 3, both)
         clip(1, 2, both)
         square(1, 2, both)
-        denominator(early0)
+        sigmoid(0, 1, 1, 2)
         clip(1, 3, (0,))
-        invert(early0)
-        clip(1, 3, (1,))
-        finish(early0)
         square(1, 3, (0,))
-        sigmoid(1, 0, 0, 2)
+        clip(1, 3, (1,))
         square(1, 3, (1,))
+        sigmoid(1, 0, 0, 2)
         sigmoid(0, 1, 2, 4)
         sigmoid(1, 0, 2, 4)
+        quant_w(1, 1, (0,))
+        quant_v(0)
+        mix(early0)
+        quant_w(1, 0, (1,))
+        quant_w(1, 1, (1,))
         quant_v(1)
         mix(early1)
-        quant_w(0, 2, both)
+        quant_w(0, 2, (0,))
+        quant_w(0, 2, (1,))
         quant_w(1, 2, both)
         mix(third)
+        denominator(early0)
         quant_w(0, 3, both)
+        mix(last0, (0,))
+        invert(early0)
         quant_w(1, 3, (0,))
-        mix(last0)
-        mix(last1, (0,))
+        mix(last0, (1,))
         denominator(early1)
-        invert(early1)
+        finish(early0)
+        mix(last1, (0,))
         quant_w(1, 3, (1,))
         mix(last1, (1,))
-        finish(early1)
+        invert(early1)
         denominator(third)
         denominator(last0)
-        denominator(last1)
+        finish(early1)
         invert(third)
         invert(last0)
-        invert(last1)
+        denominator(last1)
         finish(third)
+        invert(last1)
         finish(last0)
         finish(last1)

@@ -21,20 +21,30 @@ PASSES = N // TOK
 QC = 128
 CHUNKS = NQ // QC
 HALF = NQ // 2
-RUN = 4
+RUN = 2
+
+SCORE_BANKS = 2
+SUM_BANKS = 4
+SMALL_BUFS = 4
+
+K0_VECTOR_SHARE = 84
+K1_SCALAR_SHARE = 44
+Q_GPSIMD_SHARE = 192
+
+VECTOR, SCALAR, GPSIMD = "vector", "scalar", "gpsimd"
 
 
 def tile_rows_a_relu2_mask_gate_kernel(tc, qT, kT, t, v, mask, og, out):
     nc = tc.nc
     with ExitStack() as ctx:
         keep = ctx.enter_context(tc.tile_pool(name="keep", bufs=1))
-        work = ctx.enter_context(tc.tile_pool(name="work", bufs=4))
+        small = ctx.enter_context(tc.tile_pool(name="small", bufs=SMALL_BUFS))
         psum = ctx.enter_context(tc.psum_pool(name="psum", bufs=1))
         ctx.enter_context(tc.manual_schedule())
 
-        def load(name, shape, src, queue=nc.sync):
+        def load(name, shape, src):
             tile = keep.tile(shape, F32, name=name, align_bytes=64)
-            queue.dma_start(out=tile[:], in_=src)
+            nc.sync.dma_start(out=tile[:], in_=src)
             return tile
 
         k_src = kT.rearrange("h (p j) n -> (h p) j n", j=PACK)
@@ -43,20 +53,20 @@ def tile_rows_a_relu2_mask_gate_kernel(tc, qT, kT, t, v, mask, og, out):
         def load_k(g):
             return load("k_raw%d" % g, [P, PACK, TOK], k_src[:, :, g * TOK:(g + 1) * TOK])
 
-        def load_q(a):
-            return load("q_raw%d" % a, [P, PACK, HALF], q_src[:, :, a * HALF:(a + 1) * HALF])
+        def load_q(half):
+            return load("q_raw%d" % half, [P, PACK, HALF], q_src[:, :, half * HALF:(half + 1) * HALF])
 
-        def load_mask(g, a):
+        def load_mask(g, half):
             rows = mask[g * TOK:(g + 1) * TOK, :].rearrange("(p j) n -> p j n", j=PACK)
-            return load("m_raw%d%d" % (g, a), [P, PACK, HALF], rows[:, :, a * HALF:(a + 1) * HALF])
+            return load("m_raw%d%d" % (g, half), [P, PACK, HALF], rows[:, :, half * HALF:(half + 1) * HALF])
 
         def load_v(h):
             rows = v[h].rearrange("(g p j) e -> p g (j e)", p=P, j=PACK)
             return load("v_raw%d" % h, [P, PASSES, PACK * E], rows)
 
-        def load_og(h, c0, c1, queue=nc.sync):
+        def load_og(h, c0, c1):
             rows = og[h, c0 * QC:c1 * QC, :].rearrange("(c p) e -> p c e", p=P)
-            return load("og_raw%d%d" % (h, c0), [P, c1 - c0, E], rows, queue)
+            return load("og_raw%d%d" % (h, c0), [P, c1 - c0, E], rows)
 
         k_raw, q_raw, m_raw, v_raw, og_raw = {}, {}, {}, {}, {}
         t_raw = load("t_raw", [P, PASSES, PACK], t.rearrange("(g p j) o -> p g (j o)", p=P, j=PACK))
@@ -94,13 +104,17 @@ def tile_rows_a_relu2_mask_gate_kernel(tc, qT, kT, t, v, mask, og, out):
         nc.scalar.activation(out=t_sign[:], in_=t_all, func=ACT.Sign)
         sigmoid(0, 0, 0, 1)
         nc.vector.reciprocal(out=inv_guess[:], in_=guess[:])
-        nc.vector.scalar_tensor_tensor(out=half_ratio[:], in0=inv_guess[:], scalar=0.5, in1=t_abs[:], op0=ALU.mult, op1=ALU.mult)
-        nc.vector.scalar_tensor_tensor(out=t_root[:], in0=guess[:], scalar=0.5, in1=half_ratio[:], op0=ALU.mult, op1=ALU.add)
+        nc.vector.scalar_tensor_tensor(
+            out=half_ratio[:], in0=inv_guess[:], scalar=0.5, in1=t_abs[:], op0=ALU.mult, op1=ALU.mult
+        )
+        nc.vector.scalar_tensor_tensor(
+            out=t_root[:], in0=guess[:], scalar=0.5, in1=half_ratio[:], op0=ALU.mult, op1=ALU.add
+        )
 
         def copy_on(engine, dst, src):
-            if engine == "V":
+            if engine == VECTOR:
                 nc.vector.tensor_copy(out=dst, in_=src)
-            elif engine == "G":
+            elif engine == GPSIMD:
                 nc.gpsimd.tensor_scalar(out=dst, in0=src, scalar1=1.0, scalar2=0.0, op0=ALU.mult, op1=ALU.add)
             else:
                 nc.scalar.copy(out=dst, in_=src)
@@ -112,11 +126,11 @@ def tile_rows_a_relu2_mask_gate_kernel(tc, qT, kT, t, v, mask, og, out):
             nc.vector.quantize_mx(out=codes[:].bitcast(FP8X4), scales=scales[:], in_=packed)
             return codes, scales
 
+        def staging(name, shape, tag):
+            return keep.tile(shape, BF16, name="packed_%s" % name, tag=tag, align_bytes=64)
+
         k_packed, q_packed, v_packed = {}, {}, {}
         k_mx, q_mx, v_mx, w_mx = {}, {}, {}, {}
-
-        def staging(key, shape, tag):
-            return keep.tile(shape, BF16, name="packed_%s" % key, tag=tag, align_bytes=64)
 
         def pack_k(engine, g, s0, s1):
             if g not in k_packed:
@@ -131,56 +145,54 @@ def tile_rows_a_relu2_mask_gate_kernel(tc, qT, kT, t, v, mask, og, out):
         def pack_q(engine, c0, c1, n0, n1, tag):
             if c0 not in q_packed:
                 q_packed[c0] = staging("q%d" % c0, [P, (c1 - c0) * QC, PACK], tag)
-            a, off = divmod(c0 * QC, HALF)
-            dst = q_packed[c0][:, n0:n1, :].rearrange("p (c i) j -> p c j i", i=RUN)
-            src = q_raw[a][:, :, off + n0:off + n1].rearrange("p j (c i) -> p c j i", i=RUN)
+            half, start = divmod(c0 * QC, HALF)
+            dst = q_packed[c0][:, n0:n1, :].rearrange("p (m i) j -> p m j i", i=RUN)
+            src = q_raw[half][:, :, start + n0:start + n1].rearrange("p j (m i) -> p m j i", i=RUN)
             copy_on(engine, dst, src)
 
         def quant_q(c0, c1):
             codes, scales = quantize("q%d" % c0, q_packed[c0][:].rearrange("p n j -> p (n j)"))
             for c in range(c0, c1):
-                cols = slice((c - c0) * QC, (c - c0 + 1) * QC)
-                q_mx[c] = (codes, scales, cols)
+                q_mx[c] = (codes, scales, slice((c - c0) * QC, (c - c0 + 1) * QC))
 
         def pack_v(h, tag):
             v_packed[h] = staging("v%d" % h, [P, PASSES, E, PACK], tag)
             for g in range(PASSES):
-                dst = v_packed[h][:, g, :, :].rearrange("p (c i) j -> p c j i", i=RUN)
-                src = v_raw[h][:, g, :].rearrange("p (j c i) -> p c j i", j=PACK, i=RUN)
-                signs = t_sign[:, g * PACK:(g + 1) * PACK].unsqueeze(1).unsqueeze(3).to_broadcast([P, E // RUN, PACK, RUN])
-                nc.gpsimd.tensor_tensor(out=dst, in0=src, in1=signs, op=ALU.mult)
+                dst = v_packed[h][:, g, :, :].rearrange("p (m i) j -> p m j i", i=RUN)
+                src = v_raw[h][:, g, :].rearrange("p (j m i) -> p m j i", j=PACK, i=RUN)
+                signs = t_sign[:, g * PACK:(g + 1) * PACK].unsqueeze(1).unsqueeze(3)
+                nc.gpsimd.tensor_tensor(
+                    out=dst, in0=src, in1=signs.to_broadcast([P, E // RUN, PACK, RUN]), op=ALU.mult
+                )
 
         def quant_v(h):
             v_mx[h] = quantize("v%d" % h, v_packed[h][:].rearrange("p g e j -> p (g e j)"))
 
-        rooted = {}
+        rooted, banks, clipped, weights = {}, {}, {}, {}
 
-        def scale_mask(engine, g, c, tag=""):
-            dst = keep.tile([P, PACK, QC], F32, name="rooted%d%d" % (g, c), tag=tag, align_bytes=64)
-            a, off = divmod(c * QC, HALF)
+        def scale_mask(engine, g, c):
+            dst = keep.tile([P, PACK, QC], F32, name="rooted%d%d" % (g, c), align_bytes=64)
+            half, start = divmod(c * QC, HALF)
             for j in range(PACK):
-                src = m_raw[g, a][:, j, off:off + QC]
+                src = m_raw[g, half][:, j, start:start + QC]
                 root = t_root[:, g * PACK + j:g * PACK + j + 1]
-                if engine == "V":
+                if engine == VECTOR:
                     nc.vector.tensor_scalar(out=dst[:, j, :], in0=src, scalar1=root, scalar2=None, op0=ALU.mult)
-                elif engine == "G":
-                    nc.gpsimd.tensor_scalar(out=dst[:, j, :], in0=src, scalar1=root, scalar2=0.0, op0=ALU.mult, op1=ALU.add)
                 else:
                     nc.scalar.activation(out=dst[:, j, :], in_=src, func=ACT.Copy, scale=root)
             rooted[g, c] = dst
 
-        banks, masked, weights = {}, {}, {}
-
         def scores(g, c):
             q_codes, q_scales, cols = q_mx[c]
+            k_codes, k_scales = k_mx[g]
             for h in range(H):
-                bank = psum.tile([P, PACK, QC], F32, name="scores%d" % h, bufs=2)
+                bank = psum.tile([P, PACK, QC], F32, name="scores%d" % h, bufs=SCORE_BANKS)
                 rows = slice(h * ROWS, (h + 1) * ROWS)
                 for j in range(PACK):
                     nc.tensor.matmul_mx(
                         out=bank[:, j, :],
-                        lhsT=k_mx[g][0][rows, j * P:(j + 1) * P].bitcast(FP8X4),
-                        lhsT_scale=k_mx[g][1][rows, j * P:(j + 1) * P],
+                        lhsT=k_codes[rows, j * P:(j + 1) * P].bitcast(FP8X4),
+                        lhsT_scale=k_scales[rows, j * P:(j + 1) * P],
                         rhs=q_codes[rows, cols].bitcast(FP8X4),
                         rhs_scale=q_scales[rows, cols],
                         start=True,
@@ -188,164 +200,175 @@ def tile_rows_a_relu2_mask_gate_kernel(tc, qT, kT, t, v, mask, og, out):
                     )
                 banks[g, c, h] = bank
 
-        def clip(g, c, heads, only=None):
-            if (g, c, heads) not in masked:
-                masked[g, c, heads] = keep.tile([P, PACK, len(heads) * QC], F32, name="masked%d%d%d" % (g, c, heads[0]))
-            u = masked[g, c, heads]
-            for i, h in enumerate(heads):
-                if only is None or h == only:
-                    nc.vector.scalar_tensor_tensor(
-                        out=u[:, :, i * QC:(i + 1) * QC], in0=banks[g, c, h][:], scalar=0.0, in1=rooted[g, c][:],
-                        op0=ALU.max, op1=ALU.mult,
-                    )
+        def clip(g, c, heads, h):
+            if (g, c, heads) not in clipped:
+                clipped[g, c, heads] = keep.tile(
+                    [P, PACK, len(heads) * QC], F32, name="clipped%d%d%d" % (g, c, heads[0])
+                )
+            cols = slice(heads.index(h) * QC, (heads.index(h) + 1) * QC)
+            nc.vector.scalar_tensor_tensor(
+                out=clipped[g, c, heads][:, :, cols], in0=banks[g, c, h][:], scalar=0.0, in1=rooted[g, c][:],
+                op0=ALU.max, op1=ALU.mult,
+            )
 
-        def square(g, c, heads, engine="S"):
-            w = staging("w%d%d%d" % (g, c, heads[0]), [P, len(heads) * QC, PACK], "stage_w%d%d%d" % (g, c, heads[0]))
-            dst = w[:].rearrange("p (c i) j -> p c j i", i=RUN)
-            src = masked[g, c, heads][:].rearrange("p j (c i) -> p c j i", i=RUN)
-            if engine == "S":
-                nc.scalar.activation(out=dst, in_=src, func=ACT.Square)
-            else:
-                nc.vector.tensor_tensor(out=dst, in0=src, in1=src, op=ALU.mult)
+        def weight_tag(g, c, heads):
+            return "stage_w%d%d%d" % (g, c, heads[0])
+
+        def square(g, c, heads):
+            w = staging("w%d%d%d" % (g, c, heads[0]), [P, len(heads) * QC, PACK], weight_tag(g, c, heads))
+            nc.scalar.activation(
+                out=w[:].rearrange("p (m i) j -> p m j i", i=RUN),
+                in_=clipped[g, c, heads][:].rearrange("p j (m i) -> p m j i", i=RUN),
+                func=ACT.Square,
+            )
             weights[g, c, heads] = w
 
+        def weigh(g, c, heads):
+            for h in heads:
+                clip(g, c, heads, h)
+            square(g, c, heads)
+
         def quant_w(g, c, heads):
-            codes, scales = quantize("w%d%d%d" % (g, c, heads[0]), weights[g, c, heads][:].rearrange("p n j -> p (n j)"))
+            codes, scales = quantize(
+                "w%d%d%d" % (g, c, heads[0]), weights[g, c, heads][:].rearrange("p n j -> p (n j)")
+            )
             for i, h in enumerate(heads):
                 w_mx[g, c, h] = (codes[:, i * QC:(i + 1) * QC], scales[:, i * QC:(i + 1) * QC])
 
         sums, dens, invs = {}, {}, {}
 
-        def mix(unit, passes=range(PASSES)):
-            if unit not in sums:
-                sums[unit] = psum.tile([P, len(unit), E], F32, name="sums", bufs=4)
-            y = sums[unit]
-            for i, (c, h) in enumerate(unit):
+        def mix(group, passes=range(PASSES)):
+            if group not in sums:
+                sums[group] = psum.tile([P, len(group), E], F32, name="sums", bufs=SUM_BANKS)
+            for i, (c, h) in enumerate(group):
+                v_codes, v_scales = v_mx[h]
                 for g in passes:
+                    w_codes, w_scales = w_mx[g, c, h]
                     nc.tensor.matmul_mx(
-                        out=y[:, i, :],
-                        lhsT=w_mx[g, c, h][0].bitcast(FP8X4),
-                        lhsT_scale=w_mx[g, c, h][1],
-                        rhs=v_mx[h][0][:, g * E:(g + 1) * E].bitcast(FP8X4),
-                        rhs_scale=v_mx[h][1][:, g * E:(g + 1) * E],
+                        out=sums[group][:, i, :],
+                        lhsT=w_codes.bitcast(FP8X4),
+                        lhsT_scale=w_scales,
+                        rhs=v_codes[:, g * E:(g + 1) * E].bitcast(FP8X4),
+                        rhs_scale=v_scales[:, g * E:(g + 1) * E],
                         start=(g == 0),
                         stop=(g == PASSES - 1),
                     )
 
-        def denominator(unit):
-            den = work.tile([P, len(unit)], F32, name="den")
-            nc.vector.tensor_scalar(out=den[:], in0=sums[unit][:, :, E - 1], scalar1=1.0, scalar2=None, op0=ALU.add)
-            dens[unit] = den
+        def denominator(group):
+            den = small.tile([P, len(group)], F32, name="den")
+            nc.vector.tensor_scalar(
+                out=den[:], in0=sums[group][:, :, E - 1], scalar1=1.0, scalar2=None, op0=ALU.add
+            )
+            dens[group] = den
 
-        def invert(unit):
-            inv = work.tile([P, len(unit)], F32, name="inv")
-            nc.vector.reciprocal(out=inv[:], in_=dens[unit][:])
-            invs[unit] = inv
+        def invert(group):
+            inv = small.tile([P, len(group)], F32, name="inv")
+            nc.vector.reciprocal(out=inv[:], in_=dens[group][:])
+            invs[group] = inv
 
-        def finish(unit):
-            res = keep.tile([P, len(unit), E], F32, name="res%d%d" % unit[0])
-            for i, (c, h) in enumerate(unit):
+        def finish(group):
+            res = keep.tile([P, len(group), E], F32, name="res%d%d" % group[0])
+            for i, (c, h) in enumerate(group):
                 nc.vector.scalar_tensor_tensor(
-                    out=res[:, i, :], in0=sums[unit][:, i, :], scalar=invs[unit][:, i:i + 1], in1=gates[h, c],
+                    out=res[:, i, :], in0=sums[group][:, i, :], scalar=invs[group][:, i:i + 1], in1=gates[h, c],
                     op0=ALU.mult, op1=ALU.mult,
                 )
-            (c0, h0), (c1, h1) = unit[0], unit[-1]
+            (c0, h0), (c1, h1) = group[0], group[-1]
             if h0 == h1:
                 dst = out[h0, c0 * QC:(c1 + 1) * QC, :].rearrange("(c p) e -> p c e", p=P)
             else:
                 dst = out[:, c0 * QC:(c0 + 1) * QC, :].rearrange("h p e -> p h e")
             nc.sync.dma_start(out=dst, in_=res[:])
 
-        both = (0, 1)
+        both, head0, head1 = (0, 1), (0,), (1,)
         early0, early1 = ((0, 0), (1, 0)), ((0, 1), (1, 1))
-        third, last0, last1 = ((2, 0), (2, 1)), ((3, 0),), ((3, 1),)
-        pack_k("V", 0, 0, 84)
-        pack_k("S", 0, 84, P)
+        third = ((2, 0), (2, 1))
+        last0, last1 = ((3, 0),), ((3, 1),)
+
+
+        pack_k(VECTOR, 0, 0, K0_VECTOR_SHARE)
+        pack_k(SCALAR, 0, K0_VECTOR_SHARE, P)
         quant_k(0)
-        pack_q("S", 0, 1, 0, QC, "stage_q0")
-        pack_q("V", 1, 2, 0, QC, "stage_q1")
-        quant_q(0, 1)
-        scores(0, 0)
-        quant_q(1, 2)
-        scores(0, 1)
-        scale_mask("V", 0, 0)
-        scale_mask("S", 0, 1)
-        clip(0, 0, (0,))
-        square(0, 0, (0,))
-        clip(0, 0, (1,))
-        square(0, 0, (1,))
+        pack_q(SCALAR, 0, 1, 0, QC, "stage_q0")
+        pack_q(VECTOR, 1, 2, 0, QC, "stage_q1")
+        for c in (0, 1):
+            quant_q(c, c + 1)
+            scores(0, c)
+        scale_mask(VECTOR, 0, 0)
+        scale_mask(SCALAR, 0, 1)
+
+        weigh(0, 0, head0)
+        weigh(0, 0, head1)
         clip(0, 1, both, 0)
-        pack_k("S", 1, 0, 44)
-        pack_k("V", 1, 44, P)
-        quant_w(0, 0, (0,))
+        pack_k(SCALAR, 1, 0, K1_SCALAR_SHARE)
+        pack_k(VECTOR, 1, K1_SCALAR_SHARE, P)
+        quant_w(0, 0, head0)
         quant_k(1)
         scores(1, 0)
-        scale_mask("S", 1, 1)
-        scale_mask("V", 1, 0)
-        quant_w(0, 0, (1,))
+        scale_mask(SCALAR, 1, 1)
+        scale_mask(VECTOR, 1, 0)
+        quant_w(0, 0, head1)
+
         clip(0, 1, both, 1)
         scores(1, 1)
-        pack_q("G", 2, 4, 0, 192, "stage_k1")
-        pack_q("S", 2, 4, 192, HALF, "stage_k1")
+        pack_q(GPSIMD, 2, CHUNKS, 0, Q_GPSIMD_SHARE, weight_tag(0, 0, head1))
+        pack_q(SCALAR, 2, CHUNKS, Q_GPSIMD_SHARE, HALF, weight_tag(0, 0, head1))
         square(0, 1, both)
-        clip(1, 0, (0,))
-        square(1, 0, (0,))
-        clip(1, 0, (1,))
-        square(1, 0, (1,))
-        quant_q(2, 4)
+        weigh(1, 0, head0)
+        weigh(1, 0, head1)
+
+        quant_q(2, CHUNKS)
         scores(0, 2)
-        scale_mask("V", 0, 2)
+        scale_mask(VECTOR, 0, 2)
         quant_w(0, 1, both)
-        quant_w(1, 0, (0,))
-        pack_v(0, "stage_w010")
+        quant_w(1, 0, head0)
+
+        pack_v(0, weight_tag(0, 1, both))
         pack_v(1, "stage_v1")
-        scale_mask("S", 0, 3)
-        clip(1, 1, (0,))
-        square(1, 1, (0,))
-        clip(1, 1, (1,))
-        square(1, 1, (1,))
+        scale_mask(SCALAR, 0, 3)
+        weigh(1, 1, head0)
+        weigh(1, 1, head1)
         scores(0, 3)
-        clip(0, 2, (0,))
-        square(0, 2, (0,))
-        clip(0, 2, (1,))
+        weigh(0, 2, head0)
+        clip(0, 2, head1, 1)
         scores(1, 2)
-        scale_mask("S", 1, 2)
-        scale_mask("S", 1, 3)
-        square(0, 2, (1,))
-        clip(0, 3, both)
+        scale_mask(SCALAR, 1, 2)
+        scale_mask(SCALAR, 1, 3)
+        square(0, 2, head1)
+        clip(0, 3, both, 0)
+        clip(0, 3, both, 1)
         scores(1, 3)
         square(0, 3, both)
-        clip(1, 2, both)
-        square(1, 2, both)
+        weigh(1, 2, both)
         sigmoid(0, 1, 1, 2)
-        clip(1, 3, (0,))
-        square(1, 3, (0,))
-        clip(1, 3, (1,))
-        square(1, 3, (1,))
+        weigh(1, 3, head0)
+        weigh(1, 3, head1)
         sigmoid(1, 0, 0, 2)
-        sigmoid(0, 1, 2, 4)
-        sigmoid(1, 0, 2, 4)
-        quant_w(1, 1, (0,))
+        sigmoid(0, 1, 2, CHUNKS)
+        sigmoid(1, 0, 2, CHUNKS)
+
+        quant_w(1, 1, head0)
         quant_v(0)
         mix(early0)
-        quant_w(1, 0, (1,))
-        quant_w(1, 1, (1,))
+        quant_w(1, 0, head1)
+        quant_w(1, 1, head1)
         quant_v(1)
         mix(early1)
-        quant_w(0, 2, (0,))
-        quant_w(0, 2, (1,))
+        quant_w(0, 2, head0)
+        quant_w(0, 2, head1)
         quant_w(1, 2, both)
         mix(third)
+
         denominator(early0)
         quant_w(0, 3, both)
         mix(last0, (0,))
         invert(early0)
-        quant_w(1, 3, (0,))
+        quant_w(1, 3, head0)
         mix(last0, (1,))
         denominator(early1)
         finish(early0)
         mix(last1, (0,))
-        quant_w(1, 3, (1,))
+        quant_w(1, 3, head1)
         mix(last1, (1,))
         invert(early1)
         denominator(third)

from contextlib import ExitStack

import concourse.mybir as mybir

H, D, NQ, N, E = 2, 256, 512, 1024, 128
FLOPS = 2 * H * D * N * NQ + 2 * H * N * NQ * E

F32 = mybir.dt.float32
BF16 = mybir.dt.bfloat16
U32 = mybir.dt.uint32
U8 = mybir.dt.uint8
FP8X4 = mybir.dt.float8_e4m3fn_x4
ALU = mybir.AluOpType
ACT = mybir.ActivationFunctionType

P = 128
PACK = 4
ROWS = D // PACK
TOK = P * PACK
PASSES = N // TOK
QC = 128
CHUNKS = NQ // QC
HALF = NQ // 2
RUN = 2

SCORE_BANKS = 2
SUM_BANKS = 4
SMALL_BUFS = 4

K0_VECTOR_SHARE = 84
K1_SCALAR_SHARE = 44
Q_GPSIMD_SHARE = 192

VECTOR, SCALAR, GPSIMD = "vector", "scalar", "gpsimd"


def tile_rows_a_relu2_mask_gate_kernel(tc, qT, kT, t, v, mask, og, out):
    nc = tc.nc
    with ExitStack() as ctx:
        keep = ctx.enter_context(tc.tile_pool(name="keep", bufs=1))
        small = ctx.enter_context(tc.tile_pool(name="small", bufs=SMALL_BUFS))
        psum = ctx.enter_context(tc.psum_pool(name="psum", bufs=1))
        ctx.enter_context(tc.manual_schedule())

        def load(name, shape, src):
            tile = keep.tile(shape, F32, name=name, align_bytes=64)
            nc.sync.dma_start(out=tile[:], in_=src)
            return tile

        k_src = kT.rearrange("h (p j) n -> (h p) j n", j=PACK)
        q_src = qT.rearrange("h (p j) n -> (h p) j n", j=PACK)

        def load_k(g):
            return load("k_raw%d" % g, [P, PACK, TOK], k_src[:, :, g * TOK:(g + 1) * TOK])

        def load_q(half):
            return load("q_raw%d" % half, [P, PACK, HALF], q_src[:, :, half * HALF:(half + 1) * HALF])

        def load_mask(g, half):
            rows = mask[g * TOK:(g + 1) * TOK, :].rearrange("(p j) n -> p j n", j=PACK)
            return load("m_raw%d%d" % (g, half), [P, PACK, HALF], rows[:, :, half * HALF:(half + 1) * HALF])

        def load_v(h):
            rows = v[h].rearrange("(g p j) e -> p g (j e)", p=P, j=PACK)
            return load("v_raw%d" % h, [P, PASSES, PACK * E], rows)

        def load_og(h, c0, c1):
            rows = og[h, c0 * QC:c1 * QC, :].rearrange("(c p) e -> p c e", p=P)
            return load("og_raw%d%d" % (h, c0), [P, c1 - c0, E], rows)

        k_raw, q_raw, m_raw, v_raw, og_raw = {}, {}, {}, {}, {}
        t_raw = load("t_raw", [P, PASSES, PACK], t.rearrange("(g p j) o -> p g (j o)", p=P, j=PACK))
        og_raw[0, 0] = load_og(0, 0, 1)
        k_raw[0] = load_k(0)
        q_raw[0] = load_q(0)
        m_raw[0, 0] = load_mask(0, 0)
        k_raw[1] = load_k(1)
        m_raw[1, 0] = load_mask(1, 0)
        q_raw[1] = load_q(1)
        m_raw[0, 1] = load_mask(0, 1)
        v_raw[0] = load_v(0)
        v_raw[1] = load_v(1)
        m_raw[1, 1] = load_mask(1, 1)
        og_raw[0, 1] = load_og(0, 1, CHUNKS)
        og_raw[1, 0] = load_og(1, 0, CHUNKS)

        gates = {}

        def sigmoid(h, first, c0, c1):
            gate = keep.tile([P, c1 - c0, E], F32, name="gate%d%d" % (h, c0))
            nc.scalar.activation(out=gate[:], in_=og_raw[h, first][:, c0 - first:c1 - first, :], func=ACT.Sigmoid)
            for c in range(c0, c1):
                gates[h, c] = gate[:, c - c0, :]

        t_all = t_raw[:].rearrange("p g j -> p (g j)")
        t_abs = keep.tile([P, PASSES * PACK], F32)
        t_sign = keep.tile([P, PASSES * PACK], F32)
        guess = keep.tile([P, PASSES * PACK], F32)
        inv_guess = keep.tile([P, PASSES * PACK], F32)
        half_ratio = keep.tile([P, PASSES * PACK], F32)
        t_root = keep.tile([P, PASSES * PACK], F32)
        nc.vector.scalar_tensor_tensor(out=t_abs[:], in0=t_all, scalar=-1.0, in1=t_all, op0=ALU.mult, op1=ALU.max)
        nc.scalar.activation(out=guess[:], in_=t_abs[:], func=ACT.Sqrt)
        nc.scalar.activation(out=t_sign[:], in_=t_all, func=ACT.Sign)
        sigmoid(0, 0, 0, 1)
        nc.vector.reciprocal(out=inv_guess[:], in_=guess[:])
        nc.vector.scalar_tensor_tensor(
            out=half_ratio[:], in0=inv_guess[:], scalar=0.5, in1=t_abs[:], op0=ALU.mult, op1=ALU.mult
        )
        nc.vector.scalar_tensor_tensor(
            out=t_root[:], in0=guess[:], scalar=0.5, in1=half_ratio[:], op0=ALU.mult, op1=ALU.add
        )

        def copy_on(engine, dst, src):
            if engine == VECTOR:
                nc.vector.tensor_copy(out=dst, in_=src)
            elif engine == GPSIMD:
                nc.gpsimd.tensor_scalar(out=dst, in0=src, scalar1=1.0, scalar2=0.0, op0=ALU.mult, op1=ALU.add)
            else:
                nc.scalar.copy(out=dst, in_=src)

        def quantize(name, packed):
            width = packed.shape[1] // PACK
            codes = keep.tile([P, width], U32, name=name + "_codes", align_bytes=64)
            scales = keep.tile([P, width], U8, name=name + "_scales", align_bytes=64)
            nc.vector.quantize_mx(out=codes[:].bitcast(FP8X4), scales=scales[:], in_=packed)
            return codes, scales

        def staging(name, shape, tag):
            return keep.tile(shape, BF16, name="packed_%s" % name, tag=tag, align_bytes=64)

        k_packed, q_packed, v_packed = {}, {}, {}
        k_mx, q_mx, v_mx, w_mx = {}, {}, {}, {}

        def pack_k(engine, g, s0, s1):
            if g not in k_packed:
                k_packed[g] = staging("k%d" % g, [P, PACK, P, PACK], "stage_k%d" % g)
            dst = k_packed[g][:, :, s0:s1, :].rearrange("p r s j -> p s j r")
            src = k_raw[g][:, :, s0 * PACK:s1 * PACK].rearrange("p j (s r) -> p s j r", r=PACK)
            copy_on(engine, dst, src)

        def quant_k(g):
            k_mx[g] = quantize("k%d" % g, k_packed[g][:].rearrange("p r s j -> p (r s j)"))

        def pack_q(engine, c0, c1, n0, n1, tag):
            if c0 not in q_packed:
                q_packed[c0] = staging("q%d" % c0, [P, (c1 - c0) * QC, PACK], tag)
            half, start = divmod(c0 * QC, HALF)
            dst = q_packed[c0][:, n0:n1, :].rearrange("p (m i) j -> p m j i", i=RUN)
            src = q_raw[half][:, :, start + n0:start + n1].rearrange("p j (m i) -> p m j i", i=RUN)
            copy_on(engine, dst, src)

        def quant_q(c0, c1):
            codes, scales = quantize("q%d" % c0, q_packed[c0][:].rearrange("p n j -> p (n j)"))
            for c in range(c0, c1):
                q_mx[c] = (codes, scales, slice((c - c0) * QC, (c - c0 + 1) * QC))

        def pack_v(h, tag):
            v_packed[h] = staging("v%d" % h, [P, PASSES, E, PACK], tag)
            for g in range(PASSES):
                dst = v_packed[h][:, g, :, :].rearrange("p (m i) j -> p m j i", i=RUN)
                src = v_raw[h][:, g, :].rearrange("p (j m i) -> p m j i", j=PACK, i=RUN)
                signs = t_sign[:, g * PACK:(g + 1) * PACK].unsqueeze(1).unsqueeze(3)
                nc.gpsimd.tensor_tensor(
                    out=dst, in0=src, in1=signs.to_broadcast([P, E // RUN, PACK, RUN]), op=ALU.mult
                )

        def quant_v(h):
            v_mx[h] = quantize("v%d" % h, v_packed[h][:].rearrange("p g e j -> p (g e j)"))

        rooted, banks, clipped, weights = {}, {}, {}, {}

        def scale_mask(engine, g, c):
            dst = keep.tile([P, PACK, QC], F32, name="rooted%d%d" % (g, c), align_bytes=64)
            half, start = divmod(c * QC, HALF)
            for j in range(PACK):
                src = m_raw[g, half][:, j, start:start + QC]
                root = t_root[:, g * PACK + j:g * PACK + j + 1]
                if engine == VECTOR:
                    nc.vector.tensor_scalar(out=dst[:, j, :], in0=src, scalar1=root, scalar2=None, op0=ALU.mult)
                else:
                    nc.scalar.activation(out=dst[:, j, :], in_=src, func=ACT.Copy, scale=root)
            rooted[g, c] = dst

        def scores(g, c):
            q_codes, q_scales, cols = q_mx[c]
            k_codes, k_scales = k_mx[g]
            for h in range(H):
                bank = psum.tile([P, PACK, QC], F32, name="scores%d" % h, bufs=SCORE_BANKS)
                rows = slice(h * ROWS, (h + 1) * ROWS)
                for j in range(PACK):
                    nc.tensor.matmul_mx(
                        out=bank[:, j, :],
                        lhsT=k_codes[rows, j * P:(j + 1) * P].bitcast(FP8X4),
                        lhsT_scale=k_scales[rows, j * P:(j + 1) * P],
                        rhs=q_codes[rows, cols].bitcast(FP8X4),
                        rhs_scale=q_scales[rows, cols],
                        start=True,
                        stop=True,
                    )
                banks[g, c, h] = bank

        def clip(g, c, heads, h):
            if (g, c, heads) not in clipped:
                clipped[g, c, heads] = keep.tile(
                    [P, PACK, len(heads) * QC], F32, name="clipped%d%d%d" % (g, c, heads[0])
                )
            cols = slice(heads.index(h) * QC, (heads.index(h) + 1) * QC)
            nc.vector.scalar_tensor_tensor(
                out=clipped[g, c, heads][:, :, cols], in0=banks[g, c, h][:], scalar=0.0, in1=rooted[g, c][:],
                op0=ALU.max, op1=ALU.mult,
            )

        def weight_tag(g, c, heads):
            return "stage_w%d%d%d" % (g, c, heads[0])

        def square(g, c, heads):
            w = staging("w%d%d%d" % (g, c, heads[0]), [P, len(heads) * QC, PACK], weight_tag(g, c, heads))
            nc.scalar.activation(
                out=w[:].rearrange("p (m i) j -> p m j i", i=RUN),
                in_=clipped[g, c, heads][:].rearrange("p j (m i) -> p m j i", i=RUN),
                func=ACT.Square,
            )
            weights[g, c, heads] = w

        def weigh(g, c, heads):
            for h in heads:
                clip(g, c, heads, h)
            square(g, c, heads)

        def quant_w(g, c, heads):
            codes, scales = quantize(
                "w%d%d%d" % (g, c, heads[0]), weights[g, c, heads][:].rearrange("p n j -> p (n j)")
            )
            for i, h in enumerate(heads):
                w_mx[g, c, h] = (codes[:, i * QC:(i + 1) * QC], scales[:, i * QC:(i + 1) * QC])

        sums, dens, invs = {}, {}, {}

        def mix(group, passes=range(PASSES)):
            if group not in sums:
                sums[group] = psum.tile([P, len(group), E], F32, name="sums", bufs=SUM_BANKS)
            for i, (c, h) in enumerate(group):
                v_codes, v_scales = v_mx[h]
                for g in passes:
                    w_codes, w_scales = w_mx[g, c, h]
                    nc.tensor.matmul_mx(
                        out=sums[group][:, i, :],
                        lhsT=w_codes.bitcast(FP8X4),
                        lhsT_scale=w_scales,
                        rhs=v_codes[:, g * E:(g + 1) * E].bitcast(FP8X4),
                        rhs_scale=v_scales[:, g * E:(g + 1) * E],
                        start=(g == 0),
                        stop=(g == PASSES - 1),
                    )

        def denominator(group):
            den = small.tile([P, len(group)], F32, name="den")
            nc.vector.tensor_scalar(
                out=den[:], in0=sums[group][:, :, E - 1], scalar1=1.0, scalar2=None, op0=ALU.add
            )
            dens[group] = den

        def invert(group):
            inv = small.tile([P, len(group)], F32, name="inv")
            nc.vector.reciprocal(out=inv[:], in_=dens[group][:])
            invs[group] = inv

        def finish(group):
            res = keep.tile([P, len(group), E], F32, name="res%d%d" % group[0])
            for i, (c, h) in enumerate(group):
                nc.vector.scalar_tensor_tensor(
                    out=res[:, i, :], in0=sums[group][:, i, :], scalar=invs[group][:, i:i + 1], in1=gates[h, c],
                    op0=ALU.mult, op1=ALU.mult,
                )
            (c0, h0), (c1, h1) = group[0], group[-1]
            if h0 == h1:
                dst = out[h0, c0 * QC:(c1 + 1) * QC, :].rearrange("(c p) e -> p c e", p=P)
            else:
                dst = out[:, c0 * QC:(c0 + 1) * QC, :].rearrange("h p e -> p h e")
            nc.sync.dma_start(out=dst, in_=res[:])

        both, head0, head1 = (0, 1), (0,), (1,)
        early0, early1 = ((0, 0), (1, 0)), ((0, 1), (1, 1))
        third = ((2, 0), (2, 1))
        last0, last1 = ((3, 0),), ((3, 1),)


        pack_k(VECTOR, 0, 0, K0_VECTOR_SHARE)
        pack_k(SCALAR, 0, K0_VECTOR_SHARE, P)
        quant_k(0)
        pack_q(SCALAR, 0, 1, 0, QC, "stage_q0")
        pack_q(VECTOR, 1, 2, 0, QC, "stage_q1")
        for c in (0, 1):
            quant_q(c, c + 1)
            scores(0, c)
        scale_mask(VECTOR, 0, 0)
        scale_mask(SCALAR, 0, 1)

        weigh(0, 0, head0)
        weigh(0, 0, head1)
        clip(0, 1, both, 0)
        pack_k(SCALAR, 1, 0, K1_SCALAR_SHARE)
        pack_k(VECTOR, 1, K1_SCALAR_SHARE, P)
        quant_w(0, 0, head0)
        quant_k(1)
        scores(1, 0)
        scale_mask(SCALAR, 1, 1)
        scale_mask(VECTOR, 1, 0)
        quant_w(0, 0, head1)

        clip(0, 1, both, 1)
        scores(1, 1)
        pack_q(GPSIMD, 2, CHUNKS, 0, Q_GPSIMD_SHARE, weight_tag(0, 0, head1))
        pack_q(SCALAR, 2, CHUNKS, Q_GPSIMD_SHARE, HALF, weight_tag(0, 0, head1))
        square(0, 1, both)
        weigh(1, 0, head0)
        weigh(1, 0, head1)

        quant_q(2, CHUNKS)
        scores(0, 2)
        scale_mask(VECTOR, 0, 2)
        quant_w(0, 1, both)
        quant_w(1, 0, head0)

        pack_v(0, weight_tag(0, 1, both))
        pack_v(1, "stage_v1")
        scale_mask(SCALAR, 0, 3)
        weigh(1, 1, head0)
        weigh(1, 1, head1)
        scores(0, 3)
        weigh(0, 2, head0)
        clip(0, 2, head1, 1)
        scores(1, 2)
        scale_mask(SCALAR, 1, 2)
        scale_mask(SCALAR, 1, 3)
        square(0, 2, head1)
        clip(0, 3, both, 0)
        clip(0, 3, both, 1)
        scores(1, 3)
        square(0, 3, both)
        weigh(1, 2, both)
        sigmoid(0, 1, 1, 2)
        weigh(1, 3, head0)
        weigh(1, 3, head1)
        sigmoid(1, 0, 0, 2)
        sigmoid(0, 1, 2, CHUNKS)
        sigmoid(1, 0, 2, CHUNKS)

        quant_w(1, 1, head0)
        quant_v(0)
        mix(early0)
        quant_w(1, 0, head1)
        quant_w(1, 1, head1)
        quant_v(1)
        mix(early1)
        quant_w(0, 2, head0)
        quant_w(0, 2, head1)
        quant_w(1, 2, both)
        mix(third)

        denominator(early0)
        quant_w(0, 3, both)
        mix(last0, (0,))
        invert(early0)
        quant_w(1, 3, head0)
        mix(last0, (1,))
        denominator(early1)
        finish(early0)
        mix(last1, (0,))
        quant_w(1, 3, head1)
        mix(last1, (1,))
        invert(early1)
        denominator(third)
        denominator(last0)
        finish(early1)
        invert(third)
        invert(last0)
        denominator(last1)
        finish(third)
        invert(last1)
        finish(last0)
        finish(last1)
